import numpy as np
import ml_dtypes


def mxq(x, axis, fmt="e4m3"):
    dtype, down = {"e4m3": (ml_dtypes.float8_e4m3fn, 7), "e5m2": (ml_dtypes.float8_e5m2, 14)}[fmt]
    v = np.moveaxis(np.asarray(x, np.float32).astype(ml_dtypes.bfloat16).astype(np.float64), axis, -1)
    blocks = v.reshape(v.shape[:-1] + (-1, 32))
    amax = np.abs(blocks).max(-1, keepdims=True)
    byte = np.maximum(np.where(amax > 0, np.frexp(amax)[1] - 1 + 127, 0) - down, 1)
    scale = np.exp2(byte - 127.0)
    codes = (blocks / scale).astype(np.float32).astype(dtype).astype(np.float64)
    return np.moveaxis((codes * scale).reshape(v.shape), -1, axis)


WIDE = False


def mx_kscale(k):
    if not WIDE:
        return np.ones(k)
    levels = np.array([10, -10, 5, -5, 0])
    if k % 512:
        return np.exp2(np.random.permutation(np.resize(levels, k // 32))).repeat(32)
    a = np.empty((k // 512, 16))
    for p in range(k // 512):
        a[p, :8] = np.random.permutation(np.resize(levels, 8))
        for g in range(8):
            far = levels[np.abs(levels - a[p, g]) >= 10]
            a[p, g + 8] = far[np.random.randint(len(far))]
    return np.exp2(a.ravel()).repeat(32)


def f64(x):
    return np.asarray(x).astype(np.float64)


def striped(idx):
    return np.tile(idx.reshape(-1, 16).T, (8, 1)).astype(np.uint16)


def unstriped(offs):
    return offs[:16].T.reshape(-1).astype(np.int64)


E2M1 = np.array([0.0, 0.5, 1.0, 1.5, 2.0, 3.0, 4.0, 6.0, -0.0, -0.5, -1.0, -1.5, -2.0, -3.0, -4.0, -6.0])


def pack_weight(w, fmt):
    k, n = w.shape
    w = f64(np.asarray(w, np.float32).astype(ml_dtypes.bfloat16)).reshape(k // 32, 32, n)
    amax = np.abs(w).max(1)
    if fmt == "e4m3":
        byte = np.frexp(amax)[1] - 1 + 127 - 7
    else:
        mant, ex = np.frexp(amax / 6.0)
        byte = np.where(mant > 0.5, ex, ex - 1) + 127
    byte = np.clip(np.where(amax > 0, byte, 1), 1, 254)
    scaled = (w * np.exp2(127.0 - byte)[:, None, :]).reshape(k, n).astype(np.float32)
    by_word = np.ascontiguousarray(scaled.reshape(k // 512, 128, 4, n).transpose(0, 1, 3, 2))
    if fmt == "e4m3":
        words = by_word.astype(ml_dtypes.float8_e4m3fn).view(np.uint8)
    else:
        c = by_word.astype(ml_dtypes.float4_e2m1fn).view(np.uint8) & 0xF
        words = (c[..., 0::2] | (c[..., 1::2] << 4)).reshape(k // 512, 128, 2 * n)
    return np.ascontiguousarray(words), np.ascontiguousarray(byte.astype(np.uint8).reshape(k // 512, 16, n))


def unpack_weight(words, scales, fmt):
    g, _, n = scales.shape
    words = np.ascontiguousarray(words).reshape(g, 128, n, -1)
    if fmt == "e4m3":
        vals = words.view(ml_dtypes.float8_e4m3fn).astype(np.float64)
    else:
        nib = np.empty((g, 128, n, 4), np.uint8)
        nib[..., 0::2] = words & 0xF
        nib[..., 1::2] = words >> 4
        vals = E2M1[nib]
    vals = vals * np.repeat(np.exp2(scales.astype(np.float64) - 127.0), 8, axis=1)[..., None]
    return vals.transpose(0, 1, 3, 2).reshape(g * 512, n)


def gelu(v):
    return 0.5 * v * (1.0 + np.tanh(np.sqrt(2.0 / np.pi) * (v + 0.044715 * v**3)))


K, H, N, T, S, T2, P = 1536, 1024, 256, 4096, 1024, 2048, 1024

def setup_inputs():
    n = np.random.standard_normal
    s = mx_kscale(K)[:, None]
    u = mx_kscale(H)[:, None]
    d = {}
    d["tab_words"], d["tab_scales"] = pack_weight(n((K, T)) * s, "e4m3")
    d["offs"] = striped(np.random.permutation(T)[:S])
    d["offs2"] = striped(np.random.permutation(T2)[:S])
    d["offs3"] = striped(np.random.permutation(T2)[:P])
    d["offs4"] = striped(np.random.permutation(T2)[:P])
    d["w1"] = (0.55 * n((K, H)) / K ** 0.5 / s).astype(np.float32)
    d["gain"] = (1.2 * np.exp(0.3 * n(H)) * u[:, 0]).astype(np.float32)
    d["wgs"] = np.exp(0.3 * n((128, S))).astype(np.float32)
    d["page0"] = (0.8 * n((H, T2)) * u).astype(np.float32)
    d["base"] = (0.8 * np.exp(0.3 * n(H)) * u[:, 0]).astype(np.float32)
    d["w4_words"], d["w4_scales"] = pack_weight(n((H, N)) / H ** 0.5 / u, "e2m1")
    d["w5"] = (1.3 * n((H, N)) / H ** 0.5 / u).astype(np.float32)
    d["w6_words"], d["w6_scales"] = pack_weight(1.7 * n((H, N)) / H ** 0.5 / u, "e4m3")
    d["wgo"] = np.exp(0.3 * n((128, P))).astype(np.float32)
    d["page1"] = (0.8 * n((N, T2))).astype(np.float32)
    return d

def reference(tab_words, tab_scales, offs, offs2, offs3, offs4, w1, gain, wgs, page0, base, w4_words, w4_scales, w5, w6_words, w6_scales, wgo, page1):
    v = unpack_weight(tab_words, tab_scales, "e4m3")[:, unstriped(offs)]
    h = f64(gain)[:, None] * np.cos(mxq(f64(w1), 0, "e4m3").T @ v)
    page = f64(page0).copy()
    page[:, unstriped(offs2)] = np.tile(f64(wgs), (H // 128, 1)) * h
    x = page[:, unstriped(offs3)] - f64(base)[:, None]
    xq = mxq(x, 0, "e4m3")
    rq = mxq(np.maximum(x, 0.0), 0, "e4m3")
    y1 = unpack_weight(w4_words, w4_scales, "e2m1").T @ xq
    y2 = mxq(f64(w5), 0, "e4m3").T @ rq
    y3 = unpack_weight(w6_words, w6_scales, "e4m3").T @ xq
    y = np.maximum(np.abs(y1 - y2), y3)
    out = f64(page1).copy()
    out[:, unstriped(offs4)] = np.tile(f64(wgo), (N // 128, 1)) * y
    return out

@@ -1,0 +1,380 @@
+import math
+from contextlib import ExitStack
+
+import concourse.mybir as mybir
+from concourse.masks import make_identity
+
+K, H, N, T, S, T2, PICKS = 1536, 1024, 256, 4096, 1024, 2048, 1024
+FLOPS = 2 * K * H * S + 3 * 2 * H * N * PICKS
+
+F32 = mybir.dt.float32
+BF16 = mybir.dt.bfloat16
+I32 = mybir.dt.int32
+U32 = mybir.dt.uint32
+U16 = mybir.dt.uint16
+U8 = mybir.dt.uint8
+FP8X4 = mybir.dt.float8_e4m3fn_x4
+FP4X4 = mybir.dt.float4_e2m1fn_x4
+ALU = mybir.AluOpType
+ACT = mybir.ActivationFunctionType
+
+P = 128
+PACK = 4
+K_PASS = P * PACK
+HALF = 512
+K_PASSES = K // K_PASS
+H_PASSES = H // K_PASS
+SLICES = H // P
+KIB = 1024
+
+TURN_OFFSET = 98304.0
+TURN_OFFSET_BITS = 1203765248.0
+BITS_PER_TURN = 128.0
+
+
+def tile_list_lane_square_page_kernel(
+    tc, tab_words, tab_scales, offs, offs2, offs3, offs4, w1, gain, wgs, page0, base,
+    w4_words, w4_scales, w5, w6_words, w6_scales, wgo, page1, out,
+):
+    nc = tc.nc
+    with ExitStack() as ctx:
+        held = ctx.enter_context(tc.tile_pool(name="held", bufs=1))
+        shared = ctx.enter_context(tc.tile_pool(name="shared", bufs=1))
+        ring = ctx.enter_context(tc.tile_pool(name="ring", bufs=2))
+        psum = ctx.enter_context(tc.psum_pool(name="psum", bufs=1))
+
+        idx_tab = held.tile([P, S // 16], U16, name="idx_tab")
+        idx_put = held.tile([P, S // 16], U16, name="idx_put")
+        idx_get = held.tile([P, PICKS // 16], U16, name="idx_get")
+        idx_out = held.tile([P, PICKS // 16], U16, name="idx_out")
+
+        tab = [shared.tile([P, T], U32, name=f"tab{g}", offset=16 * KIB * g) for g in range(K_PASSES)]
+        page = [
+            shared.tile([P, T2], F32, name=f"page{s}", offset=(48 + 8 * s if s < 4 else 8 * (s - 4)) * KIB)
+            for s in range(SLICES)
+        ]
+        result = [shared.tile([P, T2], F32, name=f"result{b}", offset=(32 + 8 * b) * KIB) for b in range(N // P)]
+        tab_sc = shared.tile([P, T], U8, name="tab_sc", offset=80 * KIB)
+        wgo_sb = shared.tile([P, PICKS], F32, name="wgo_sb", offset=80 * KIB)
+
+        v_words = [held.tile([P, S], U32, name=f"v_words{g}", align_bytes=64) for g in range(K_PASSES)]
+        v_sc = held.tile([P, S], U8, name="v_sc", align_bytes=64)
+        w1_codes = [[held.tile([P, K_PASS], U32, name=f"w1_codes{a}{g}", align_bytes=64) for g in range(K_PASSES)]
+                    for a in range(H_PASSES)]
+        w1_sc = [[held.tile([P, K_PASS], U8, name=f"w1_sc{a}{g}", align_bytes=64) for g in range(K_PASSES)]
+                 for a in range(H_PASSES)]
+        wgs_first = held.tile([P, S], F32, name="wgs_first")
+        wgs_rest = held.tile([P, PACK - 1, S], F32, name="wgs_rest")
+        gain_sb = held.tile([P, H_PASSES, PACK], F32, name="gain_sb")
+        base_sb = held.tile([P, H_PASSES, PACK], F32, name="base_sb")
+        neg_base = held.tile([P, H_PASSES, PACK], F32, name="neg_base")
+        w4_sb = held.tile([P, H_PASSES * 2 * N], U8, name="w4_sb", align_bytes=64)
+        w6_sb = held.tile([P, H_PASSES * N], U32, name="w6_sb", align_bytes=64)
+        w4_sc = held.tile([P, H_PASSES * N], U8, name="w4_sc", align_bytes=64)
+        w6_sc = held.tile([P, H_PASSES * N], U8, name="w6_sc", align_bytes=64)
+        w5_codes = held.tile([P, H_PASSES * N], U32, name="w5_codes", align_bytes=64)
+        w5_sc = held.tile([P, H_PASSES * N], U8, name="w5_sc", align_bytes=64)
+        ident = held.tile([P, P], F32, name="ident")
+        minus_offset = held.tile([P, P], F32, name="minus_offset")
+        work = [held.tile([P, HALF], F32, name=f"work{n}") for n in range(4)]
+        spare = held.tile([P, HALF], F32, name="spare")
+        zero_in = held.tile([P, 1], F32, name="zero_in")
+        zero = held.tile([P, 1], F32, name="zero")
+
+        def x_tiles(a, h):
+            if a == 0:
+                return (
+                    held.tile([P, HALF], U32, name=f"xq{a}{h}", align_bytes=64),
+                    held.tile([P, HALF], U8, name=f"xs{a}{h}", align_bytes=64),
+                    held.tile([P, HALF], U32, name=f"rq{a}{h}", align_bytes=64),
+                    held.tile([P, HALF], U8, name=f"rs{a}{h}", align_bytes=64),
+                )
+            at = (48 + 8 * h) * KIB
+            return (
+                shared.tile([P, HALF], U32, name=f"xq{a}{h}", offset=at, align_bytes=64),
+                shared.tile([P, HALF], U8, name=f"xs{a}{h}", offset=at + 2 * KIB, align_bytes=64),
+                shared.tile([P, HALF], U32, name=f"rq{a}{h}", offset=at + 3 * KIB, align_bytes=64),
+                shared.tile([P, HALF], U8, name=f"rs{a}{h}", offset=at + 5 * KIB, align_bytes=64),
+            )
+
+        x_mx = {(a, h): x_tiles(a, h) for a in range(H_PASSES) for h in range(2)}
+
+        def bank(i):
+            return psum.tile([P, HALF], F32, name=f"bank{i}", tag=f"bank{i}")
+
+        nc.gpsimd.memset(zero_in[:], 0.0)
+        nc.scalar.activation(zero[:], zero_in[:], ACT.Sin)
+        nc.vector.memset(tab_sc[:].bitcast(I32), 0)
+        nc.vector.memset(w4_sc[:].bitcast(I32), 0)
+        nc.vector.memset(w6_sc[:].bitcast(I32), 0)
+        nc.vector.memset(minus_offset[:], -TURN_OFFSET)
+
+        w1_raw = {}
+
+        def load_w1(a, g):
+            raw = ring.tile([P, PACK, K_PASS], F32, name="raw", tag="raw", bufs=3)
+            rows = w1[g * K_PASS:(g + 1) * K_PASS, a * K_PASS:(a + 1) * K_PASS]
+            nc.sync.dma_start(raw[:], rows.rearrange("(p i) c -> p i c", i=PACK))
+            w1_raw[a, g] = raw
+
+        def load_tab(g):
+            nc.sync.dma_start(tab[g][:].bitcast(I32), tab_words[g].rearrange("p n i -> p (n i)").bitcast(I32))
+
+        def load_page(s):
+            a, t = divmod(s, PACK)
+            rows = page0[a * K_PASS:(a + 1) * K_PASS, :].rearrange("(p i) m -> p i m", i=PACK)
+            nc.sync.dma_start(page[s][:], rows[:, t, :])
+
+        wgs_rows = wgs.rearrange("(q i) j -> q i j", i=PACK)
+
+        nc.sync.dma_start(idx_tab[:], offs)
+        make_identity(nc, ident[:])
+        load_tab(0)
+        for q in range(4):
+            nc.sync.dma_start(tab_sc[32 * q:32 * q + 4 * K_PASSES, :].bitcast(I32),
+                              tab_scales[:, 4 * q:4 * q + 4, :].bitcast(I32))
+        load_w1(0, 0)
+        load_w1(0, 1)
+        load_tab(1)
+        load_w1(0, 2)
+        load_tab(2)
+        nc.sync.dma_start(gain_sb[:], gain.rearrange("(a p i) -> p a i", p=P, i=PACK))
+        nc.sync.dma_start(idx_put[:], offs2)
+        for q in range(4):
+            nc.sync.dma_start(wgs_first[32 * q:32 * (q + 1), :], wgs_rows[:, 0, :])
+        load_page(0)
+        for q in range(4):
+            nc.sync.dma_start(wgs_rest[32 * q:32 * (q + 1), :, :], wgs_rows[:, 1:, :])
+        load_page(1)
+        for g in range(K_PASSES):
+            load_w1(1, g)
+        nc.sync.dma_start(idx_get[:], offs3)
+        nc.sync.dma_start(base_sb[:], base.rearrange("(a p i) -> p a i", p=P, i=PACK))
+        load_page(2)
+        load_page(3)
+
+        def gather_words(g, c0, c1):
+            nc.vector.tensor_copy(v_words[g][:, c0:c1], tab[g][:].indirect(idx_tab[:, c0 // 16:c1 // 16]))
+
+        staged = {}
+
+        def staging(key):
+            if key not in staged:
+                staged[key] = ring.tile([P, K_PASS * PACK], BF16, name="grouped", tag="grouped", bufs=3, align_bytes=64)
+            return staged[key]
+
+        follows = {(1, HALF): ("w1", 1, 0), (2, 0): ("w1", 1, 1), (2, HALF): ("w1", 1, 2),
+                   (5, HALF): "w5", (6, HALF): ("x", 0, 0), (7, HALF): ("x", 0, 1)}
+
+        def cast_w1(a, g):
+            grouped = staging(("w1", a, g))
+            nc.scalar.copy(grouped[:].rearrange("p (t m i) -> p m t i", t=PACK, i=PACK),
+                           w1_raw[a, g][:].rearrange("p i (m t) -> p m t i", t=PACK))
+
+        def quantize_w1(a, g):
+            nc.vector.quantize_mx(w1_codes[a][g][:].bitcast(FP8X4), w1_sc[a][g][:], staging(("w1", a, g))[:])
+
+        new_states = {}
+
+        def scratch(s, role):
+            return work[(role + 3 * s) % 4]
+
+        def first_product(s, c0, c1, z, angle, whole):
+            a, t = divmod(s, PACK)
+            blocks = (c1 - c0) // P
+            for g in range(K_PASSES):
+                for b in range(blocks):
+                    cols = slice(c0 + b * P, c0 + (b + 1) * P)
+                    nc.tensor.matmul_mx(
+                        out=z[:, b * P:(b + 1) * P],
+                        lhsT=v_words[g][:, cols].bitcast(FP8X4),
+                        lhsT_scale=v_sc[4 * g:P, cols],
+                        rhs=w1_codes[a][g][:, t * P:(t + 1) * P].bitcast(FP8X4),
+                        rhs_scale=w1_sc[a][g][:, t * P:(t + 1) * P],
+                        start=(g == 0 and b == 0),
+                        stop=(g == K_PASSES - 1 and b == blocks - 1),
+                    )
+            if (s, c0) == (0, HALF):
+                nc.vector.tensor_scalar(angle, z[:, :c1 - c0], 1.0 / (2.0 * math.pi), 0.25, ALU.mult, ALU.add)
+                nc.vector.tensor_scalar(whole.bitcast(I32), angle, -BITS_PER_TURN, TURN_OFFSET_BITS, ALU.mult, ALU.add)
+            else:
+                nc.scalar.activation(angle, z[:, :c1 - c0], ACT.Copy, bias=0.25, scale=1.0 / (2.0 * math.pi))
+                nc.scalar.activation(whole.bitcast(U32), angle, ACT.Copy, bias=TURN_OFFSET_BITS, scale=-BITS_PER_TURN)
+
+        def cosine(s, c0, c1, frac, angle, whole):
+            a, t = divmod(s, PACK)
+            blocks = (c1 - c0) // P
+            terms = [[minus_offset[:]] * blocks,
+                     [whole[:, b * P:(b + 1) * P] for b in range(blocks)],
+                     [angle[:, b * P:(b + 1) * P] for b in range(blocks)]]
+            for n, term in enumerate(terms):
+                for b in range(blocks):
+                    nc.tensor.matmul(frac[:, b * P:(b + 1) * P], term[b], ident[:], is_transpose=True,
+                                     start=(n == 0 and b == 0), stop=(n == len(terms) - 1 and b == blocks - 1))
+            if (s, c0) in follows:
+                wave = staging(follows[s, c0])[:].bitcast(F32)[:, :c1 - c0]
+            else:
+                wave = ring.tile([P, HALF], F32, name="wave", tag="wave")[:, :c1 - c0]
+            nc.scalar.activation(wave, frac[:, :c1 - c0], ACT.Sin, bias=zero[:], scale=2.0 * math.pi)
+            nc.scalar.activation(new_states[s][:, c0:c1], wave, ACT.Copy, scale=gain_sb[:, a, t:t + 1])
+
+        def states(s, pieces):
+            new_states[s] = ring.tile([P, S], F32, name="new_state", tag="new_state")
+            jobs = []
+            for c0, c1, z_bank, frac_bank in pieces:
+                h, at = divmod(c0, HALF)
+                angle = scratch(s, 3 * h)[:, at:at + c1 - c0]
+                whole = scratch(s, 1 + h)[:, at:at + c1 - c0]
+                first_product(s, c0, c1, bank(z_bank), angle, whole)
+                jobs.append((c0, c1, frac_bank, angle, whole))
+            for c0, c1, frac_bank, angle, whole in jobs:
+                cosine(s, c0, c1, bank(frac_bank), angle, whole)
+
+        def put(s, c0=0, c1=S):
+            t = s % PACK
+            rows = wgs_first[:, c0:c1] if t == 0 else wgs_rest[:, t - 1, c0:c1]
+            nc.vector.tensor_tensor(page[s][:].indirect(idx_put[:, c0 // 16:c1 // 16]),
+                                    new_states[s][:, c0:c1], rows, ALU.mult)
+
+        picked = {}
+        rounded = {}
+
+        def get(s, h, into):
+            picked[s, h] = into
+            nc.vector.tensor_copy(into, page[s][:].indirect(idx_get[:, h * 32:(h + 1) * 32]))
+
+        def depart(s, h):
+            a, t = divmod(s, PACK)
+            if t == 0:
+                rounded[a, h] = ring.tile([P, PACK, HALF], BF16, name="rounded", tag="rounded", bufs=3)
+            nc.scalar.activation(rounded[a, h][:, t, :], picked[s, h], ACT.Identity, bias=neg_base[:, a, t:t + 1])
+
+        woven = {}
+
+        def weave(a, h):
+            x_bf = staging(("x", a, h))
+            nc.scalar.copy(x_bf[:].rearrange("p (c i t) -> p c t i", i=4, t=PACK),
+                           rounded[a, h][:].rearrange("p t (c i) -> p c t i", i=4))
+            woven[a, h] = x_bf
+
+        def quantize_x(a, h):
+            xq, xs, rq, rs = x_mx[a, h]
+            r_bf = ring.tile([P, HALF * PACK], BF16, name="raised", tag="raised", align_bytes=64)
+            nc.vector.tensor_scalar_max(r_bf[:], woven[a, h][:], 0.0)
+            nc.vector.quantize_mx(xq[:].bitcast(FP8X4), xs[:], woven[a, h][:])
+            nc.vector.quantize_mx(rq[:].bitcast(FP8X4), rs[:], r_bf[:])
+
+        sums = {}
+
+        def second_products(a, h, b):
+            if a == 0:
+                first = 4 * (1 - h) + 2 * b
+                sums[h, b] = (bank(first), bank(first + 1))
+            diff, third = sums[h, b]
+            xq, xs, rq, rs = x_mx[a, h]
+            cols = slice(a * N + b * P, a * N + (b + 1) * P)
+            w4_cols = slice(2 * cols.start, 2 * cols.stop)
+            last = a == H_PASSES - 1
+            nc.tensor.matmul_mx(out=diff[:], lhsT=w4_sb[:, w4_cols].bitcast(FP4X4), lhsT_scale=w4_sc[:, cols],
+                                rhs=xq[:].bitcast(FP8X4), rhs_scale=xs[:], start=(a == 0), stop=False)
+            nc.tensor.matmul_mx(out=diff[:], lhsT=w5_codes[:, cols].bitcast(FP8X4), lhsT_scale=w5_sc[:, cols],
+                                rhs=rq[:].bitcast(FP8X4), rhs_scale=rs[:], start=False, stop=last)
+            nc.tensor.matmul_mx(out=third[:], lhsT=w6_sb[:, cols].bitcast(FP8X4), lhsT_scale=w6_sc[:, cols],
+                                rhs=xq[:].bitcast(FP8X4), rhs_scale=xs[:], start=(a == 0), stop=last)
+
+        def score(h, b):
+            diff, third = sums[h, b]
+            gap = ring.tile([P, HALF], F32, name="gap", tag="gap")
+            y = ring.tile([P, HALF], F32, name="y", tag="y")
+            nc.scalar.activation(gap[:], diff[:], ACT.Abs, bias=zero[:])
+            nc.vector.tensor_tensor(y[:], gap[:], third[:], ALU.max)
+            nc.vector.tensor_tensor(result[b][:].indirect(idx_out[:, h * 32:(h + 1) * 32]),
+                                    y[:], wgo_sb[:, h * HALF:(h + 1) * HALF], ALU.mult)
+
+        gather_words(0, 0, S)
+        cast_w1(0, 0)
+        nc.vector.tensor_copy(v_sc[:], tab_sc[:].indirect(idx_tab[:]))
+        cast_w1(0, 1)
+        quantize_w1(0, 0)
+        gather_words(1, 0, S)
+        quantize_w1(0, 1)
+        cast_w1(0, 2)
+        quantize_w1(0, 2)
+        gather_words(2, 0, HALF)
+        gather_words(2, HALF, S)
+        nc.scalar.activation(neg_base[:], base_sb[:], ACT.Copy, scale=-1.0)
+
+        for s in range(PACK, SLICES):
+            load_page(s)
+        w5_raw = ring.tile([P, H_PASSES, PACK, N], F32, name="raw", tag="raw", bufs=3)
+        nc.sync.dma_start(w5_raw[:], w5.rearrange("(a p i) n -> p a i n", p=P, i=PACK))
+        nc.sync.dma_start(w4_sb[:].bitcast(I32).rearrange("p (a c) -> p a c", a=H_PASSES),
+                          w4_words.bitcast(I32).rearrange("a p c -> p a c"))
+        nc.sync.dma_start(w6_sb[:].bitcast(I32).rearrange("p (a c) -> p a c", a=H_PASSES),
+                          w6_words.rearrange("a p c i -> p a (c i)").bitcast(I32))
+        for q in range(4):
+            for plane, scales in ((w4_sc, w4_scales), (w6_sc, w6_scales)):
+                nc.sync.dma_start(
+                    plane[32 * q:32 * q + 4, :].bitcast(I32).rearrange("r (a n) -> r a n", a=H_PASSES),
+                    scales[:, 4 * q:4 * q + 4, :].bitcast(I32).rearrange("a r n -> r a n"))
+        nc.sync.dma_start(idx_out[:], offs4)
+        nc.sync.dma_start(wgo_sb[:], wgo)
+        for b in range(N // P):
+            nc.sync.dma_start(result[b][:], page1[b * P:(b + 1) * P, :])
+
+        halves_of_list = [(0, HALF, 0, 2), (HALF, S, 1, 3)]
+        first_pieces = [(0, HALF // 2, 4, 5), (HALF // 2, HALF, 6, 7), (HALF, S, 1, 3)]
+        states(0, first_pieces)
+        for c0, c1, z_bank, frac_bank in first_pieces:
+            put(0, c0, c1)
+        states(1, halves_of_list)
+        cast_w1(1, 0)
+        for s in range(1, SLICES):
+            put(s)
+            if s + 1 < SLICES:
+                states(s + 1, halves_of_list)
+            if s == 1:
+                cast_w1(1, 1)
+                cast_w1(1, 2)
+                for g in range(K_PASSES):
+                    quantize_w1(1, g)
+            if s == PACK:
+                w5_bf = staging("w5")
+                for a in range(H_PASSES):
+                    nc.scalar.activation(
+                        w5_bf[:, a * N * PACK:(a + 1) * N * PACK].rearrange("p (n i) -> p n i", i=PACK),
+                        w5_raw[:, a, :, :].rearrange("p i n -> p n i"), ACT.Copy, scale=-1.0)
+                nc.vector.quantize_mx(w5_codes[:].bitcast(FP8X4), w5_sc[:], w5_bf[:])
+            if s == PACK + 1:
+                weave(0, 0)
+            if s == PACK + 2:
+                weave(0, 1)
+                quantize_x(0, 0)
+            halves = (0, 1) if s - 1 < PACK else (0,)
+            for h in halves:
+                get(s - 1, h, scratch(s + 1, 3 - h)[:])
+                depart(s - 1, h)
+        get(SLICES - 1, 0, spare[:])
+        depart(SLICES - 1, 0)
+        weave(1, 0)
+        quantize_x(0, 1)
+        for h in range(2):
+            for b in range(N // P):
+                second_products(0, h, b)
+        freed = [new_states[SLICES - 1][:, c:c + HALF] for c in (0, HALF)]
+        freed.extend(scratch(SLICES - 1, role)[:] for role in (0, 1))
+        for s in range(PACK, SLICES):
+            get(s, 1, freed[s - PACK])
+            depart(s, 1)
+        quantize_x(1, 0)
+        weave(1, 1)
+        for b in range(N // P):
+            second_products(1, 0, b)
+        quantize_x(1, 1)
+        for b in range(N // P):
+            second_products(1, 1, b)
+        for h in range(2):
+            for b in range(N // P):
+                score(h, b)
+        for b in range(N // P):
+            nc.sync.dma_start(out[b * P:(b + 1) * P, :], result[b][:])

@@ -55,16 +55,16 @@ def tile_list_lane_square_page_kernel(
         ]
         result = [shared.tile([P, T2], F32, name=f"result{b}", offset=(32 + 8 * b) * KIB) for b in range(N // P)]
         tab_sc = shared.tile([P, T], U8, name="tab_sc", offset=80 * KIB)
-        wgo_sb = shared.tile([P, PICKS], F32, name="wgo_sb", offset=80 * KIB)
+        wgo_sb = held.tile([P, PICKS], F32, name="wgo_sb")
 
-        v_words = [held.tile([P, S], U32, name=f"v_words{g}", align_bytes=64) for g in range(K_PASSES)]
+        v_words = [shared.tile([P, S], U32, name=f"v_words{g}", offset=(84, 80, 88)[g] * KIB, align_bytes=64)
+                   for g in range(K_PASSES)]
         v_sc = held.tile([P, S], U8, name="v_sc", align_bytes=64)
         w1_codes = [[held.tile([P, K_PASS], U32, name=f"w1_codes{a}{g}", align_bytes=64) for g in range(K_PASSES)]
                     for a in range(H_PASSES)]
         w1_sc = [[held.tile([P, K_PASS], U8, name=f"w1_sc{a}{g}", align_bytes=64) for g in range(K_PASSES)]
                  for a in range(H_PASSES)]
-        wgs_first = held.tile([P, S], F32, name="wgs_first")
-        wgs_rest = held.tile([P, PACK - 1, S], F32, name="wgs_rest")
+        wgs_sb = [shared.tile([P, S], F32, name=f"wgs{t}", offset=(92 + 4 * t) * KIB) for t in range(PACK)]
         gain_sb = held.tile([P, H_PASSES, PACK], F32, name="gain_sb")
         base_sb = held.tile([P, H_PASSES, PACK], F32, name="base_sb")
         neg_base = held.tile([P, H_PASSES, PACK], F32, name="neg_base")
@@ -77,21 +77,14 @@ def tile_list_lane_square_page_kernel(
         ident = held.tile([P, P], F32, name="ident")
         minus_offset = held.tile([P, P], F32, name="minus_offset")
         work = [held.tile([P, HALF], F32, name=f"work{n}") for n in range(4)]
-        spare = held.tile([P, HALF], F32, name="spare")
         zero_in = held.tile([P, 1], F32, name="zero_in")
         zero = held.tile([P, 1], F32, name="zero")
 
         def x_tiles(a, h):
-            if a == 0:
-                return (
-                    held.tile([P, HALF], U32, name=f"xq{a}{h}", align_bytes=64),
-                    held.tile([P, HALF], U8, name=f"xs{a}{h}", align_bytes=64),
-                    held.tile([P, HALF], U32, name=f"rq{a}{h}", align_bytes=64),
-                    held.tile([P, HALF], U8, name=f"rs{a}{h}", align_bytes=64),
-                )
-            at = (48 + 8 * h) * KIB
+            at = (48 + 8 * (2 * a + h)) * KIB
+            codes_at = (112 + 2 * h) * KIB if a == 0 else at
             return (
-                shared.tile([P, HALF], U32, name=f"xq{a}{h}", offset=at, align_bytes=64),
+                shared.tile([P, HALF], U32, name=f"xq{a}{h}", offset=codes_at, align_bytes=64),
                 shared.tile([P, HALF], U8, name=f"xs{a}{h}", offset=at + 2 * KIB, align_bytes=64),
                 shared.tile([P, HALF], U32, name=f"rq{a}{h}", offset=at + 3 * KIB, align_bytes=64),
                 shared.tile([P, HALF], U8, name=f"rs{a}{h}", offset=at + 5 * KIB, align_bytes=64),
@@ -103,8 +96,9 @@ def tile_list_lane_square_page_kernel(
             return psum.tile([P, HALF], F32, name=f"bank{i}", tag=f"bank{i}")
 
         nc.gpsimd.memset(zero_in[:], 0.0)
+        nc.gpsimd.memset(tab_sc[:, :T // 2].bitcast(I32), 0)
+        nc.vector.memset(tab_sc[:, T // 2:].bitcast(I32), 0)
         nc.scalar.activation(zero[:], zero_in[:], ACT.Sin)
-        nc.vector.memset(tab_sc[:].bitcast(I32), 0)
         nc.vector.memset(w4_sc[:].bitcast(I32), 0)
         nc.vector.memset(w6_sc[:].bitcast(I32), 0)
         nc.vector.memset(minus_offset[:], -TURN_OFFSET)
@@ -125,32 +119,36 @@ def tile_list_lane_square_page_kernel(
             rows = page0[a * K_PASS:(a + 1) * K_PASS, :].rearrange("(p i) m -> p i m", i=PACK)
             nc.sync.dma_start(page[s][:], rows[:, t, :])
 
-        wgs_rows = wgs.rearrange("(q i) j -> q i j", i=PACK)
+        def load_wgs(t):
+            rows = wgs.rearrange("(q i) j -> q i j", i=PACK)[:, t, :]
+            for q in (0, 2, 1, 3):
+                nc.sync.dma_start(wgs_sb[t][32 * q:32 * (q + 1), :], rows)
 
         nc.sync.dma_start(idx_tab[:], offs)
         make_identity(nc, ident[:])
+        load_w1(0, 0)
         load_tab(0)
+        nc.sync.dma_start(gain_sb[:], gain.rearrange("(a p i) -> p a i", p=P, i=PACK))
         for q in range(4):
             nc.sync.dma_start(tab_sc[32 * q:32 * q + 4 * K_PASSES, :].bitcast(I32),
                               tab_scales[:, 4 * q:4 * q + 4, :].bitcast(I32))
-        load_w1(0, 0)
         load_w1(0, 1)
         load_tab(1)
         load_w1(0, 2)
         load_tab(2)
-        nc.sync.dma_start(gain_sb[:], gain.rearrange("(a p i) -> p a i", p=P, i=PACK))
         nc.sync.dma_start(idx_put[:], offs2)
-        for q in range(4):
-            nc.sync.dma_start(wgs_first[32 * q:32 * (q + 1), :], wgs_rows[:, 0, :])
+        load_wgs(0)
         load_page(0)
-        for q in range(4):
-            nc.sync.dma_start(wgs_rest[32 * q:32 * (q + 1), :, :], wgs_rows[:, 1:, :])
+        load_wgs(1)
         load_page(1)
-        for g in range(K_PASSES):
-            load_w1(1, g)
+        load_w1(1, 0)
         nc.sync.dma_start(idx_get[:], offs3)
         nc.sync.dma_start(base_sb[:], base.rearrange("(a p i) -> p a i", p=P, i=PACK))
+        load_w1(1, 1)
+        load_wgs(2)
         load_page(2)
+        load_w1(1, 2)
+        load_wgs(3)
         load_page(3)
 
         def gather_words(g, c0, c1):
@@ -163,8 +161,8 @@ def tile_list_lane_square_page_kernel(
                 staged[key] = ring.tile([P, K_PASS * PACK], BF16, name="grouped", tag="grouped", bufs=3, align_bytes=64)
             return staged[key]
 
-        follows = {(1, HALF): ("w1", 1, 0), (2, 0): ("w1", 1, 1), (2, HALF): ("w1", 1, 2),
-                   (5, HALF): "w5", (6, HALF): ("x", 0, 0), (7, HALF): ("x", 0, 1)}
+        follows = {(2, 0): ("w1", 1, 0), (3, 0): ("w1", 1, 2),
+                   (5, 0): "w5", (6, 0): ("x", 0, 0), (7, 0): ("x", 0, 1)}
 
         def cast_w1(a, g):
             grouped = staging(("w1", a, g))
@@ -175,6 +173,7 @@ def tile_list_lane_square_page_kernel(
             nc.vector.quantize_mx(w1_codes[a][g][:].bitcast(FP8X4), w1_sc[a][g][:], staging(("w1", a, g))[:])
 
         new_states = {}
+        factors = {}
 
         def scratch(s, role):
             return work[(role + 3 * s) % 4]
@@ -202,39 +201,37 @@ def tile_list_lane_square_page_kernel(
                 nc.scalar.activation(whole.bitcast(U32), angle, ACT.Copy, bias=TURN_OFFSET_BITS, scale=-BITS_PER_TURN)
 
         def cosine(s, c0, c1, frac, angle, whole):
-            a, t = divmod(s, PACK)
             blocks = (c1 - c0) // P
-            terms = [[minus_offset[:]] * blocks,
-                     [whole[:, b * P:(b + 1) * P] for b in range(blocks)],
-                     [angle[:, b * P:(b + 1) * P] for b in range(blocks)]]
-            for n, term in enumerate(terms):
-                for b in range(blocks):
-                    nc.tensor.matmul(frac[:, b * P:(b + 1) * P], term[b], ident[:], is_transpose=True,
-                                     start=(n == 0 and b == 0), stop=(n == len(terms) - 1 and b == blocks - 1))
-            if (s, c0) in follows:
-                wave = staging(follows[s, c0])[:].bitcast(F32)[:, :c1 - c0]
-            else:
-                wave = ring.tile([P, HALF], F32, name="wave", tag="wave")[:, :c1 - c0]
-            nc.scalar.activation(wave, frac[:, :c1 - c0], ACT.Sin, bias=zero[:], scale=2.0 * math.pi)
-            nc.scalar.activation(new_states[s][:, c0:c1], wave, ACT.Copy, scale=gain_sb[:, a, t:t + 1])
+            terms = [(b, minus_offset[:]) for b in range(blocks)]
+            terms.extend((b, term[:, b * P:(b + 1) * P]) for b in range(blocks) for term in (whole, angle))
+            for n, (b, term) in enumerate(terms):
+                nc.tensor.matmul(frac[:, b * P:(b + 1) * P], term, ident[:], is_transpose=True,
+                                 start=(n == 0), stop=(n == len(terms) - 1))
+            nc.scalar.activation(new_states[s][:, c0:c1], frac[:, :c1 - c0], ACT.Sin, bias=zero[:], scale=2.0 * math.pi)
 
         def states(s, pieces):
-            new_states[s] = ring.tile([P, S], F32, name="new_state", tag="new_state")
+            new_states[s] = ring.tile([P, S], F32, name="new_state", tag="new_state", align_bytes=64)
+            a, t = divmod(s, PACK)
+            factors[s] = shared.tile([P, S], F32, name=f"factor{s}", offset=(108 + 4 * (s % 2)) * KIB)
+            nc.gpsimd.tensor_scalar(factors[s][:], wgs_sb[t][:], gain_sb[:, a, t:t + 1], 0.0, ALU.mult, ALU.add)
             jobs = []
             for c0, c1, z_bank, frac_bank in pieces:
                 h, at = divmod(c0, HALF)
                 angle = scratch(s, 3 * h)[:, at:at + c1 - c0]
-                whole = scratch(s, 1 + h)[:, at:at + c1 - c0]
+                if (s, c0) == (2, 0):
+                    angle = staging(("w1", 1, 1))[:].bitcast(F32)[:, :c1 - c0]
+                if (s, c0) in follows:
+                    whole = staging(follows[s, c0])[:].bitcast(F32)[:, :c1 - c0]
+                else:
+                    whole = scratch(s, 1 + h)[:, at:at + c1 - c0]
                 first_product(s, c0, c1, bank(z_bank), angle, whole)
                 jobs.append((c0, c1, frac_bank, angle, whole))
             for c0, c1, frac_bank, angle, whole in jobs:
                 cosine(s, c0, c1, bank(frac_bank), angle, whole)
 
         def put(s, c0=0, c1=S):
-            t = s % PACK
-            rows = wgs_first[:, c0:c1] if t == 0 else wgs_rest[:, t - 1, c0:c1]
             nc.vector.tensor_tensor(page[s][:].indirect(idx_put[:, c0 // 16:c1 // 16]),
-                                    new_states[s][:, c0:c1], rows, ALU.mult)
+                                    new_states[s][:, c0:c1], factors[s][:, c0:c1], ALU.mult)
 
         picked = {}
         rounded = {}
@@ -246,7 +243,7 @@ def tile_list_lane_square_page_kernel(
         def depart(s, h):
             a, t = divmod(s, PACK)
             if t == 0:
-                rounded[a, h] = ring.tile([P, PACK, HALF], BF16, name="rounded", tag="rounded", bufs=3)
+                rounded[a, h] = ring.tile([P, PACK, HALF], BF16, name="rounded", tag="rounded", bufs=4)
             nc.scalar.activation(rounded[a, h][:, t, :], picked[s, h], ACT.Identity, bias=neg_base[:, a, t:t + 1])
 
         woven = {}
@@ -259,10 +256,13 @@ def tile_list_lane_square_page_kernel(
 
         def quantize_x(a, h):
             xq, xs, rq, rs = x_mx[a, h]
-            r_bf = ring.tile([P, HALF * PACK], BF16, name="raised", tag="raised", align_bytes=64)
-            nc.vector.tensor_scalar_max(r_bf[:], woven[a, h][:], 0.0)
+            if (a, h) == (0, 0):
+                r_bf = new_states[SLICES - 1][:].bitcast(BF16)
+            else:
+                r_bf = ring.tile([P, HALF * PACK], BF16, name="raised", tag="raised", align_bytes=64)[:]
+            nc.vector.tensor_scalar_max(r_bf, woven[a, h][:], 0.0)
             nc.vector.quantize_mx(xq[:].bitcast(FP8X4), xs[:], woven[a, h][:])
-            nc.vector.quantize_mx(rq[:].bitcast(FP8X4), rs[:], r_bf[:])
+            nc.vector.quantize_mx(rq[:].bitcast(FP8X4), rs[:], r_bf)
 
         sums = {}
 
@@ -302,7 +302,7 @@ def tile_list_lane_square_page_kernel(
         quantize_w1(0, 2)
         gather_words(2, 0, HALF)
         gather_words(2, HALF, S)
-        nc.scalar.activation(neg_base[:], base_sb[:], ACT.Copy, scale=-1.0)
+        nc.gpsimd.tensor_scalar(neg_base[:], base_sb[:], -1.0, 0.0, ALU.mult, ALU.add)
 
         for s in range(PACK, SLICES):
             load_page(s)
@@ -322,57 +322,52 @@ def tile_list_lane_square_page_kernel(
         for b in range(N // P):
             nc.sync.dma_start(result[b][:], page1[b * P:(b + 1) * P, :])
 
-        halves_of_list = [(0, HALF, 0, 2), (HALF, S, 1, 3)]
+        def halves_of_list(s):
+            return [(h * HALF, (h + 1) * HALF, h + 2 * (s % 2), h + 2 * ((s + 1) % 2)) for h in range(2)]
+
         first_pieces = [(0, HALF // 2, 4, 5), (HALF // 2, HALF, 6, 7), (HALF, S, 1, 3)]
         states(0, first_pieces)
         for c0, c1, z_bank, frac_bank in first_pieces:
             put(0, c0, c1)
-        states(1, halves_of_list)
-        cast_w1(1, 0)
+        states(1, halves_of_list(1))
         for s in range(1, SLICES):
             put(s)
             if s + 1 < SLICES:
-                states(s + 1, halves_of_list)
+                states(s + 1, halves_of_list(s + 1))
             if s == 1:
+                cast_w1(1, 0)
                 cast_w1(1, 1)
+                quantize_w1(1, 0)
+                quantize_w1(1, 1)
+            if s == 2:
                 cast_w1(1, 2)
-                for g in range(K_PASSES):
-                    quantize_w1(1, g)
+                quantize_w1(1, 2)
             if s == PACK:
                 w5_bf = staging("w5")
-                for a in range(H_PASSES):
-                    nc.scalar.activation(
-                        w5_bf[:, a * N * PACK:(a + 1) * N * PACK].rearrange("p (n i) -> p n i", i=PACK),
-                        w5_raw[:, a, :, :].rearrange("p i n -> p n i"), ACT.Copy, scale=-1.0)
+                nc.scalar.activation(w5_bf[:].rearrange("p (a n i) -> p a n i", a=H_PASSES, i=PACK),
+                                     w5_raw[:].rearrange("p a i n -> p a n i"), ACT.Copy, scale=-1.0)
                 nc.vector.quantize_mx(w5_codes[:].bitcast(FP8X4), w5_sc[:], w5_bf[:])
             if s == PACK + 1:
                 weave(0, 0)
             if s == PACK + 2:
                 weave(0, 1)
-                quantize_x(0, 0)
-            halves = (0, 1) if s - 1 < PACK else (0,)
-            for h in halves:
-                get(s - 1, h, scratch(s + 1, 3 - h)[:])
-                depart(s - 1, h)
-        get(SLICES - 1, 0, spare[:])
-        depart(SLICES - 1, 0)
-        weave(1, 0)
-        quantize_x(0, 1)
+            if s + 1 < SLICES:
+                for h in range(2):
+                    get(s - 1, h, scratch(s + 1, 3 - h)[:])
+                    depart(s - 1, h)
         for h in range(2):
+            get(SLICES - 2, h, scratch(SLICES - 1, 3 - h)[:])
+            depart(SLICES - 2, h)
+            get(SLICES - 1, h, scratch(SLICES - 1, h)[:])
+            depart(SLICES - 1, h)
+            weave(1, h)
+            quantize_x(h, 0)
             for b in range(N // P):
-                second_products(0, h, b)
-        freed = [new_states[SLICES - 1][:, c:c + HALF] for c in (0, HALF)]
-        freed.extend(scratch(SLICES - 1, role)[:] for role in (0, 1))
-        for s in range(PACK, SLICES):
-            get(s, 1, freed[s - PACK])
-            depart(s, 1)
-        quantize_x(1, 0)
-        weave(1, 1)
-        for b in range(N // P):
-            second_products(1, 0, b)
-        quantize_x(1, 1)
-        for b in range(N // P):
-            second_products(1, 1, b)
+                second_products(h, 0, b)
+        for a in range(H_PASSES):
+            quantize_x(a, 1)
+            for b in range(N // P):
+                second_products(a, 1, b)
         for h in range(2):
             for b in range(N // P):
                 score(h, b)

@@ -60,8 +60,10 @@ def tile_list_lane_square_page_kernel(
         v_words = [shared.tile([P, S], U32, name=f"v_words{g}", offset=(84, 80, 88)[g] * KIB, align_bytes=64)
                    for g in range(K_PASSES)]
         v_sc = held.tile([P, S], U8, name="v_sc", align_bytes=64)
-        w1_codes = [[held.tile([P, K_PASS], U32, name=f"w1_codes{a}{g}", align_bytes=64) for g in range(K_PASSES)]
-                    for a in range(H_PASSES)]
+        w1_codes = [[held.tile([P, K_PASS], U32, name=f"w1_codes{a}{g}", align_bytes=64)
+                     if a == 0 else
+                     shared.tile([P, K_PASS], U32, name=f"w1_codes{a}{g}", offset=(48, 54, 62)[g] * KIB, align_bytes=64)
+                     for g in range(K_PASSES)] for a in range(H_PASSES)]
         w1_sc = [[held.tile([P, K_PASS], U8, name=f"w1_sc{a}{g}", align_bytes=64) for g in range(K_PASSES)]
                  for a in range(H_PASSES)]
         wgs_sb = [shared.tile([P, S], F32, name=f"wgs{t}", offset=(92 + 4 * t) * KIB) for t in range(PACK)]
@@ -72,7 +74,7 @@ def tile_list_lane_square_page_kernel(
         w6_sb = held.tile([P, H_PASSES * N], U32, name="w6_sb", align_bytes=64)
         w4_sc = held.tile([P, H_PASSES * N], U8, name="w4_sc", align_bytes=64)
         w6_sc = held.tile([P, H_PASSES * N], U8, name="w6_sc", align_bytes=64)
-        w5_codes = held.tile([P, H_PASSES * N], U32, name="w5_codes", align_bytes=64)
+        w5_codes = shared.tile([P, H_PASSES * N], U32, name="w5_codes", offset=(48 + 8 * 3 + 6) * KIB, align_bytes=64)
         w5_sc = held.tile([P, H_PASSES * N], U8, name="w5_sc", align_bytes=64)
         ident = held.tile([P, P], F32, name="ident")
         minus_offset = held.tile([P, P], F32, name="minus_offset")
@@ -82,7 +84,7 @@ def tile_list_lane_square_page_kernel(
 
         def x_tiles(a, h):
             at = (48 + 8 * (2 * a + h)) * KIB
-            codes_at = (112 + 2 * h) * KIB if a == 0 else at
+            codes_at = (104 + 2 * h) * KIB if a == 0 else at
             return (
                 shared.tile([P, HALF], U32, name=f"xq{a}{h}", offset=codes_at, align_bytes=64),
                 shared.tile([P, HALF], U8, name=f"xs{a}{h}", offset=at + 2 * KIB, align_bytes=64),
@@ -161,19 +163,18 @@ def tile_list_lane_square_page_kernel(
                 staged[key] = ring.tile([P, K_PASS * PACK], BF16, name="grouped", tag="grouped", bufs=3, align_bytes=64)
             return staged[key]
 
-        follows = {(2, 0): ("w1", 1, 0), (3, 0): ("w1", 1, 2),
-                   (5, 0): "w5", (6, 0): ("x", 0, 0), (7, 0): ("x", 0, 1)}
+        follows = {(1, HALF): ("w1", 1, 0), (2, 0): ("w1", 1, 1), (3, 0): ("w1", 1, 2),
+                   (5, 0): "w5", (6, 0): ("x", 0, 0), (7, HALF): ("x", 0, 1)}
 
         def cast_w1(a, g):
             grouped = staging(("w1", a, g))
-            nc.scalar.copy(grouped[:].rearrange("p (t m i) -> p m t i", t=PACK, i=PACK),
-                           w1_raw[a, g][:].rearrange("p i (m t) -> p m t i", t=PACK))
+            nc.scalar.copy(grouped[:].rearrange("p (t m i) -> p m i t", t=PACK, i=PACK),
+                           w1_raw[a, g][:].rearrange("p i (m t) -> p m i t", t=PACK))
 
         def quantize_w1(a, g):
             nc.vector.quantize_mx(w1_codes[a][g][:].bitcast(FP8X4), w1_sc[a][g][:], staging(("w1", a, g))[:])
 
         new_states = {}
-        factors = {}
 
         def scratch(s, role):
             return work[(role + 3 * s) % 4]
@@ -201,29 +202,27 @@ def tile_list_lane_square_page_kernel(
                 nc.scalar.activation(whole.bitcast(U32), angle, ACT.Copy, bias=TURN_OFFSET_BITS, scale=-BITS_PER_TURN)
 
         def cosine(s, c0, c1, frac, angle, whole):
+            a, t = divmod(s, PACK)
             blocks = (c1 - c0) // P
             terms = [(b, minus_offset[:]) for b in range(blocks)]
             terms.extend((b, term[:, b * P:(b + 1) * P]) for b in range(blocks) for term in (whole, angle))
             for n, (b, term) in enumerate(terms):
                 nc.tensor.matmul(frac[:, b * P:(b + 1) * P], term, ident[:], is_transpose=True,
                                  start=(n == 0), stop=(n == len(terms) - 1))
-            nc.scalar.activation(new_states[s][:, c0:c1], frac[:, :c1 - c0], ACT.Sin, bias=zero[:], scale=2.0 * math.pi)
+            if (s, c0) in follows:
+                wave = staging(follows[s, c0])[:].bitcast(F32)[:, :c1 - c0]
+            else:
+                wave = ring.tile([P, HALF], F32, name="wave", tag="wave")[:, :c1 - c0]
+            nc.scalar.activation(wave, frac[:, :c1 - c0], ACT.Sin, bias=zero[:], scale=2.0 * math.pi)
+            nc.scalar.activation(new_states[s][:, c0:c1], wave, ACT.Copy, scale=gain_sb[:, a, t:t + 1])
 
         def states(s, pieces):
             new_states[s] = ring.tile([P, S], F32, name="new_state", tag="new_state", align_bytes=64)
-            a, t = divmod(s, PACK)
-            factors[s] = shared.tile([P, S], F32, name=f"factor{s}", offset=(108 + 4 * (s % 2)) * KIB)
-            nc.gpsimd.tensor_scalar(factors[s][:], wgs_sb[t][:], gain_sb[:, a, t:t + 1], 0.0, ALU.mult, ALU.add)
             jobs = []
             for c0, c1, z_bank, frac_bank in pieces:
                 h, at = divmod(c0, HALF)
                 angle = scratch(s, 3 * h)[:, at:at + c1 - c0]
-                if (s, c0) == (2, 0):
-                    angle = staging(("w1", 1, 1))[:].bitcast(F32)[:, :c1 - c0]
-                if (s, c0) in follows:
-                    whole = staging(follows[s, c0])[:].bitcast(F32)[:, :c1 - c0]
-                else:
-                    whole = scratch(s, 1 + h)[:, at:at + c1 - c0]
+                whole = scratch(s, 1 + h)[:, at:at + c1 - c0]
                 first_product(s, c0, c1, bank(z_bank), angle, whole)
                 jobs.append((c0, c1, frac_bank, angle, whole))
             for c0, c1, frac_bank, angle, whole in jobs:
@@ -231,7 +230,7 @@ def tile_list_lane_square_page_kernel(
 
         def put(s, c0=0, c1=S):
             nc.vector.tensor_tensor(page[s][:].indirect(idx_put[:, c0 // 16:c1 // 16]),
-                                    new_states[s][:, c0:c1], factors[s][:, c0:c1], ALU.mult)
+                                    new_states[s][:, c0:c1], wgs_sb[s % PACK][:, c0:c1], ALU.mult)
 
         picked = {}
         rounded = {}
@@ -260,7 +259,7 @@ def tile_list_lane_square_page_kernel(
                 r_bf = new_states[SLICES - 1][:].bitcast(BF16)
             else:
                 r_bf = ring.tile([P, HALF * PACK], BF16, name="raised", tag="raised", align_bytes=64)[:]
-            nc.vector.tensor_scalar_max(r_bf, woven[a, h][:], 0.0)
+            nc.vector.tensor_scalar(r_bf, woven[a, h][:], -1.0, 0.0, ALU.mult, ALU.min)
             nc.vector.quantize_mx(xq[:].bitcast(FP8X4), xs[:], woven[a, h][:])
             nc.vector.quantize_mx(rq[:].bitcast(FP8X4), rs[:], r_bf)
 
@@ -323,38 +322,39 @@ def tile_list_lane_square_page_kernel(
             nc.sync.dma_start(result[b][:], page1[b * P:(b + 1) * P, :])
 
         def halves_of_list(s):
-            return [(h * HALF, (h + 1) * HALF, h + 2 * (s % 2), h + 2 * ((s + 1) % 2)) for h in range(2)]
+            return [(h * HALF, (h + 1) * HALF, h + 2 * (2 * s % 3), h + 2 * ((2 * s + 1) % 3)) for h in range(2)]
 
-        first_pieces = [(0, HALF // 2, 4, 5), (HALF // 2, HALF, 6, 7), (HALF, S, 1, 3)]
+        first_pieces = [(0, HALF // 2, 0, 2), (HALF // 2, HALF, 6, 7), (HALF, S, 1, 3)]
         states(0, first_pieces)
         for c0, c1, z_bank, frac_bank in first_pieces:
             put(0, c0, c1)
         states(1, halves_of_list(1))
+        cast_w1(1, 0)
         for s in range(1, SLICES):
             put(s)
             if s + 1 < SLICES:
                 states(s + 1, halves_of_list(s + 1))
             if s == 1:
-                cast_w1(1, 0)
                 cast_w1(1, 1)
-                quantize_w1(1, 0)
-                quantize_w1(1, 1)
             if s == 2:
                 cast_w1(1, 2)
-                quantize_w1(1, 2)
             if s == PACK:
                 w5_bf = staging("w5")
-                nc.scalar.activation(w5_bf[:].rearrange("p (a n i) -> p a n i", a=H_PASSES, i=PACK),
-                                     w5_raw[:].rearrange("p a i n -> p a n i"), ACT.Copy, scale=-1.0)
-                nc.vector.quantize_mx(w5_codes[:].bitcast(FP8X4), w5_sc[:], w5_bf[:])
-            if s == PACK + 1:
-                weave(0, 0)
-            if s == PACK + 2:
-                weave(0, 1)
+                nc.scalar.copy(w5_bf[:].rearrange("p (a c k i) -> p a c i k", a=H_PASSES, k=4, i=PACK),
+                               w5_raw[:].rearrange("p a i (c k) -> p a c i k", k=4))
+            if s in (PACK + 1, PACK + 2):
+                weave(0, s - PACK - 1)
             if s + 1 < SLICES:
                 for h in range(2):
                     get(s - 1, h, scratch(s + 1, 3 - h)[:])
                     depart(s - 1, h)
+            if s == 1:
+                quantize_w1(1, 0)
+                quantize_w1(1, 1)
+            if s == 2:
+                quantize_w1(1, 2)
+            if s == PACK:
+                nc.vector.quantize_mx(w5_codes[:].bitcast(FP8X4), w5_sc[:], staging("w5")[:])
         for h in range(2):
             get(SLICES - 2, h, scratch(SLICES - 1, 3 - h)[:])
             depart(SLICES - 2, h)

@@ -121,16 +121,20 @@ def tile_list_lane_square_page_kernel(
             rows = page0[a * K_PASS:(a + 1) * K_PASS, :].rearrange("(p i) m -> p i m", i=PACK)
             nc.sync.dma_start(page[s][:], rows[:, t, :])
 
-        def load_wgs(t):
-            rows = wgs.rearrange("(q i) j -> q i j", i=PACK)[:, t, :]
+        def load_wgs(t, c0=0, c1=S):
+            rows = wgs.rearrange("(q i) j -> q i j", i=PACK)[:, t, c0:c1]
             for q in (0, 2, 1, 3):
-                nc.sync.dma_start(wgs_sb[t][32 * q:32 * (q + 1), :], rows)
+                nc.sync.dma_start(wgs_sb[t][32 * q:32 * (q + 1), c0:c1], rows)
 
         nc.sync.dma_start(idx_tab[:], offs)
         make_identity(nc, ident[:])
+        nc.sync.dma_start(idx_put[:], offs2)
+        nc.sync.dma_start(idx_get[:], offs3)
+        nc.sync.dma_start(idx_out[:], offs4)
+        nc.sync.dma_start(gain_sb[:], gain.rearrange("(a p i) -> p a i", p=P, i=PACK))
+        nc.sync.dma_start(base_sb[:], base.rearrange("(a p i) -> p a i", p=P, i=PACK))
         load_w1(0, 0)
         load_tab(0)
-        nc.sync.dma_start(gain_sb[:], gain.rearrange("(a p i) -> p a i", p=P, i=PACK))
         for q in range(4):
             nc.sync.dma_start(tab_sc[32 * q:32 * q + 4 * K_PASSES, :].bitcast(I32),
                               tab_scales[:, 4 * q:4 * q + 4, :].bitcast(I32))
@@ -138,14 +142,12 @@ def tile_list_lane_square_page_kernel(
         load_tab(1)
         load_w1(0, 2)
         load_tab(2)
-        nc.sync.dma_start(idx_put[:], offs2)
-        load_wgs(0)
+        load_wgs(0, 0, HALF)
         load_page(0)
+        load_wgs(0, HALF, S)
         load_wgs(1)
         load_page(1)
         load_w1(1, 0)
-        nc.sync.dma_start(idx_get[:], offs3)
-        nc.sync.dma_start(base_sb[:], base.rearrange("(a p i) -> p a i", p=P, i=PACK))
         load_w1(1, 1)
         load_wgs(2)
         load_page(2)
@@ -281,14 +283,18 @@ def tile_list_lane_square_page_kernel(
             nc.tensor.matmul_mx(out=third[:], lhsT=w6_sb[:, cols].bitcast(FP8X4), lhsT_scale=w6_sc[:, cols],
                                 rhs=xq[:].bitcast(FP8X4), rhs_scale=xs[:], start=(a == 0), stop=last)
 
+        scores = {}
+
         def score(h, b):
             diff, third = sums[h, b]
             gap = ring.tile([P, HALF], F32, name="gap", tag="gap")
-            y = ring.tile([P, HALF], F32, name="y", tag="y")
+            scores[h, b] = ring.tile([P, HALF], F32, name="y", tag="y", bufs=3)
             nc.scalar.activation(gap[:], diff[:], ACT.Abs, bias=zero[:])
-            nc.vector.tensor_tensor(y[:], gap[:], third[:], ALU.max)
+            nc.vector.tensor_tensor(scores[h, b][:], gap[:], third[:], ALU.max)
+
+        def put_score(h, b):
             nc.vector.tensor_tensor(result[b][:].indirect(idx_out[:, h * 32:(h + 1) * 32]),
-                                    y[:], wgo_sb[:, h * HALF:(h + 1) * HALF], ALU.mult)
+                                    scores[h, b][:], wgo_sb[:, h * HALF:(h + 1) * HALF], ALU.mult)
 
         gather_words(0, 0, S)
         cast_w1(0, 0)
@@ -301,7 +307,7 @@ def tile_list_lane_square_page_kernel(
         quantize_w1(0, 2)
         gather_words(2, 0, HALF)
         gather_words(2, HALF, S)
-        nc.gpsimd.tensor_scalar(neg_base[:], base_sb[:], -1.0, 0.0, ALU.mult, ALU.add)
+        nc.vector.tensor_scalar(neg_base[:], base_sb[:], -1.0, 0.0, ALU.mult, ALU.add)
 
         for s in range(PACK, SLICES):
             load_page(s)
@@ -316,7 +322,6 @@ def tile_list_lane_square_page_kernel(
                 nc.sync.dma_start(
                     plane[32 * q:32 * q + 4, :].bitcast(I32).rearrange("r (a n) -> r a n", a=H_PASSES),
                     scales[:, 4 * q:4 * q + 4, :].bitcast(I32).rearrange("a r n -> r a n"))
-        nc.sync.dma_start(idx_out[:], offs4)
         nc.sync.dma_start(wgo_sb[:], wgo)
         for b in range(N // P):
             nc.sync.dma_start(result[b][:], page1[b * P:(b + 1) * P, :])
@@ -368,8 +373,11 @@ def tile_list_lane_square_page_kernel(
             quantize_x(a, 1)
             for b in range(N // P):
                 second_products(a, 1, b)
-        for h in range(2):
-            for b in range(N // P):
-                score(h, b)
+        parts = [(h, b) for h in range(2) for b in range(N // P)]
+        score(*parts[0])
+        for n, part in enumerate(parts):
+            if n + 1 < len(parts):
+                score(*parts[n + 1])
+            put_score(*part)
         for b in range(N // P):
             nc.sync.dma_start(out[b * P:(b + 1) * P, :], result[b][:])

@@ -61,7 +61,7 @@ def tile_list_lane_square_page_kernel(
                    for g in range(K_PASSES)]
         v_sc = held.tile([P, S], U8, name="v_sc", align_bytes=64)
         w1_codes = [[held.tile([P, K_PASS], U32, name=f"w1_codes{a}{g}", align_bytes=64)
-                     if a == 0 else
+                     if a == 0 or g == K_PASSES - 1 else
                      shared.tile([P, K_PASS], U32, name=f"w1_codes{a}{g}", offset=(48, 54, 62)[g] * KIB, align_bytes=64)
                      for g in range(K_PASSES)] for a in range(H_PASSES)]
         w1_sc = [[held.tile([P, K_PASS], U8, name=f"w1_sc{a}{g}", align_bytes=64) for g in range(K_PASSES)]
@@ -84,7 +84,7 @@ def tile_list_lane_square_page_kernel(
 
         def x_tiles(a, h):
             at = (48 + 8 * (2 * a + h)) * KIB
-            codes_at = (104 + 2 * h) * KIB if a == 0 else at
+            codes_at = (112 + 2 * h) * KIB if a == 0 else at
             return (
                 shared.tile([P, HALF], U32, name=f"xq{a}{h}", offset=codes_at, align_bytes=64),
                 shared.tile([P, HALF], U8, name=f"xs{a}{h}", offset=at + 2 * KIB, align_bytes=64),
@@ -165,8 +165,8 @@ def tile_list_lane_square_page_kernel(
                 staged[key] = ring.tile([P, K_PASS * PACK], BF16, name="grouped", tag="grouped", bufs=3, align_bytes=64)
             return staged[key]
 
-        follows = {(1, HALF): ("w1", 1, 0), (2, 0): ("w1", 1, 1), (3, 0): ("w1", 1, 2),
-                   (5, 0): "w5", (6, 0): ("x", 0, 0), (7, HALF): ("x", 0, 1)}
+        follows = {(2, 0): ("w1", 1, 0), (3, 0): ("w1", 1, 2),
+                   (5, 0): "w5", (6, 0): ("x", 0, 0), (7, 0): ("x", 0, 1)}
 
         def cast_w1(a, g):
             grouped = staging(("w1", a, g))
@@ -177,6 +177,7 @@ def tile_list_lane_square_page_kernel(
             nc.vector.quantize_mx(w1_codes[a][g][:].bitcast(FP8X4), w1_sc[a][g][:], staging(("w1", a, g))[:])
 
         new_states = {}
+        factors = {}
 
         def scratch(s, role):
             return work[(role + 3 * s) % 4]
@@ -204,27 +205,31 @@ def tile_list_lane_square_page_kernel(
                 nc.scalar.activation(whole.bitcast(U32), angle, ACT.Copy, bias=TURN_OFFSET_BITS, scale=-BITS_PER_TURN)
 
         def cosine(s, c0, c1, frac, angle, whole):
-            a, t = divmod(s, PACK)
             blocks = (c1 - c0) // P
             terms = [(b, minus_offset[:]) for b in range(blocks)]
             terms.extend((b, term[:, b * P:(b + 1) * P]) for b in range(blocks) for term in (whole, angle))
             for n, (b, term) in enumerate(terms):
                 nc.tensor.matmul(frac[:, b * P:(b + 1) * P], term, ident[:], is_transpose=True,
                                  start=(n == 0), stop=(n == len(terms) - 1))
-            if (s, c0) in follows:
-                wave = staging(follows[s, c0])[:].bitcast(F32)[:, :c1 - c0]
-            else:
-                wave = ring.tile([P, HALF], F32, name="wave", tag="wave")[:, :c1 - c0]
-            nc.scalar.activation(wave, frac[:, :c1 - c0], ACT.Sin, bias=zero[:], scale=2.0 * math.pi)
-            nc.scalar.activation(new_states[s][:, c0:c1], wave, ACT.Copy, scale=gain_sb[:, a, t:t + 1])
+            nc.scalar.activation(new_states[s][:, c0:c1], frac[:, :c1 - c0], ACT.Sin, bias=zero[:], scale=2.0 * math.pi)
 
         def states(s, pieces):
             new_states[s] = ring.tile([P, S], F32, name="new_state", tag="new_state", align_bytes=64)
+            a, t = divmod(s, PACK)
+            factors[s] = shared.tile([P, S], F32, name=f"factor{s}", offset=(108 + 4 * (s % 2)) * KIB)
+            for c0, c1 in ((0, HALF), (HALF, S)) if s == 0 else ((0, S),):
+                nc.gpsimd.tensor_scalar(factors[s][:, c0:c1], wgs_sb[t][:, c0:c1], gain_sb[:, a, t:t + 1], 0.0,
+                                        ALU.mult, ALU.add)
             jobs = []
             for c0, c1, z_bank, frac_bank in pieces:
                 h, at = divmod(c0, HALF)
                 angle = scratch(s, 3 * h)[:, at:at + c1 - c0]
-                whole = scratch(s, 1 + h)[:, at:at + c1 - c0]
+                if (s, c0) == (2, 0):
+                    angle = staging(("w1", 1, 1))[:].bitcast(F32)[:, :c1 - c0]
+                if (s, c0) in follows:
+                    whole = staging(follows[s, c0])[:].bitcast(F32)[:, :c1 - c0]
+                else:
+                    whole = scratch(s, 1 + h)[:, at:at + c1 - c0]
                 first_product(s, c0, c1, bank(z_bank), angle, whole)
                 jobs.append((c0, c1, frac_bank, angle, whole))
             for c0, c1, frac_bank, angle, whole in jobs:
@@ -232,7 +237,7 @@ def tile_list_lane_square_page_kernel(
 
         def put(s, c0=0, c1=S):
             nc.vector.tensor_tensor(page[s][:].indirect(idx_put[:, c0 // 16:c1 // 16]),
-                                    new_states[s][:, c0:c1], wgs_sb[s % PACK][:, c0:c1], ALU.mult)
+                                    new_states[s][:, c0:c1], factors[s][:, c0:c1], ALU.mult)
 
         picked = {}
         rounded = {}
@@ -334,12 +339,12 @@ def tile_list_lane_square_page_kernel(
         for c0, c1, z_bank, frac_bank in first_pieces:
             put(0, c0, c1)
         states(1, halves_of_list(1))
-        cast_w1(1, 0)
         for s in range(1, SLICES):
             put(s)
             if s + 1 < SLICES:
                 states(s + 1, halves_of_list(s + 1))
             if s == 1:
+                cast_w1(1, 0)
                 cast_w1(1, 1)
             if s == 2:
                 cast_w1(1, 2)

import math
from contextlib import ExitStack

import concourse.mybir as mybir
from concourse.masks import make_identity

K, H, N, T, S, T2, PICKS = 1536, 1024, 256, 4096, 1024, 2048, 1024
FLOPS = 2 * K * H * S + 3 * 2 * H * N * PICKS

F32 = mybir.dt.float32
BF16 = mybir.dt.bfloat16
I32 = mybir.dt.int32
U32 = mybir.dt.uint32
U16 = mybir.dt.uint16
U8 = mybir.dt.uint8
FP8X4 = mybir.dt.float8_e4m3fn_x4
FP4X4 = mybir.dt.float4_e2m1fn_x4
ALU = mybir.AluOpType
ACT = mybir.ActivationFunctionType

P = 128
PACK = 4
K_PASS = P * PACK
HALF = 512
K_PASSES = K // K_PASS
H_PASSES = H // K_PASS
SLICES = H // P
KIB = 1024

TURN_OFFSET = 98304.0
TURN_OFFSET_BITS = 1203765248.0
BITS_PER_TURN = 128.0


def tile_list_lane_square_page_kernel(
    tc, tab_words, tab_scales, offs, offs2, offs3, offs4, w1, gain, wgs, page0, base,
    w4_words, w4_scales, w5, w6_words, w6_scales, wgo, page1, out,
):
    nc = tc.nc
    with ExitStack() as ctx:
        held = ctx.enter_context(tc.tile_pool(name="held", bufs=1))
        shared = ctx.enter_context(tc.tile_pool(name="shared", bufs=1))
        ring = ctx.enter_context(tc.tile_pool(name="ring", bufs=2))
        psum = ctx.enter_context(tc.psum_pool(name="psum", bufs=1))

        idx_tab = held.tile([P, S // 16], U16, name="idx_tab")
        idx_put = held.tile([P, S // 16], U16, name="idx_put")
        idx_get = held.tile([P, PICKS // 16], U16, name="idx_get")
        idx_out = held.tile([P, PICKS // 16], U16, name="idx_out")

        tab = [shared.tile([P, T], U32, name=f"tab{g}", offset=16 * KIB * g) for g in range(K_PASSES)]
        page = [
            shared.tile([P, T2], F32, name=f"page{s}", offset=(48 + 8 * s if s < 4 else 8 * (s - 4)) * KIB)
            for s in range(SLICES)
        ]
        result = [shared.tile([P, T2], F32, name=f"result{b}", offset=(32 + 8 * b) * KIB) for b in range(N // P)]
        tab_sc = shared.tile([P, T], U8, name="tab_sc", offset=80 * KIB)
        wgo_sb = held.tile([P, PICKS], F32, name="wgo_sb")

        v_words = [shared.tile([P, S], U32, name=f"v_words{g}", offset=(84, 80, 88)[g] * KIB, align_bytes=64)
                   for g in range(K_PASSES)]
        v_sc = held.tile([P, S], U8, name="v_sc", align_bytes=64)
        w1_codes = [[held.tile([P, K_PASS], U32, name=f"w1_codes{a}{g}", align_bytes=64)
                     if a == 0 or g == K_PASSES - 1 else
                     shared.tile([P, K_PASS], U32, name=f"w1_codes{a}{g}", offset=(48, 54, 62)[g] * KIB, align_bytes=64)
                     for g in range(K_PASSES)] for a in range(H_PASSES)]
        w1_sc = [[held.tile([P, K_PASS], U8, name=f"w1_sc{a}{g}", align_bytes=64) for g in range(K_PASSES)]
                 for a in range(H_PASSES)]
        wgs_sb = [shared.tile([P, S], F32, name=f"wgs{t}", offset=(92 + 4 * t) * KIB) for t in range(PACK)]
        gain_sb = held.tile([P, H_PASSES, PACK], F32, name="gain_sb")
        base_sb = held.tile([P, H_PASSES, PACK], F32, name="base_sb")
        neg_base = held.tile([P, H_PASSES, PACK], F32, name="neg_base")
        w4_sb = held.tile([P, H_PASSES * 2 * N], U8, name="w4_sb", align_bytes=64)
        w6_sb = held.tile([P, H_PASSES * N], U32, name="w6_sb", align_bytes=64)
        w4_sc = held.tile([P, H_PASSES * N], U8, name="w4_sc", align_bytes=64)
        w6_sc = held.tile([P, H_PASSES * N], U8, name="w6_sc", align_bytes=64)
        w5_codes = shared.tile([P, H_PASSES * N], U32, name="w5_codes", offset=(48 + 8 * 3 + 6) * KIB, align_bytes=64)
        w5_sc = held.tile([P, H_PASSES * N], U8, name="w5_sc", align_bytes=64)
        ident = held.tile([P, P], F32, name="ident")
        minus_offset = held.tile([P, P], F32, name="minus_offset")
        work = [held.tile([P, HALF], F32, name=f"work{n}") for n in range(4)]
        zero_in = held.tile([P, 1], F32, name="zero_in")
        zero = held.tile([P, 1], F32, name="zero")

        def x_tiles(a, h):
            at = (48 + 8 * (2 * a + h)) * KIB
            codes_at = (112 + 2 * h) * KIB if a == 0 else at
            return (
                shared.tile([P, HALF], U32, name=f"xq{a}{h}", offset=codes_at, align_bytes=64),
                shared.tile([P, HALF], U8, name=f"xs{a}{h}", offset=at + 2 * KIB, align_bytes=64),
                shared.tile([P, HALF], U32, name=f"rq{a}{h}", offset=at + 3 * KIB, align_bytes=64),
                shared.tile([P, HALF], U8, name=f"rs{a}{h}", offset=at + 5 * KIB, align_bytes=64),
            )

        x_mx = {(a, h): x_tiles(a, h) for a in range(H_PASSES) for h in range(2)}

        def bank(i):
            return psum.tile([P, HALF], F32, name=f"bank{i}", tag=f"bank{i}")

        nc.gpsimd.memset(zero_in[:], 0.0)
        nc.gpsimd.memset(tab_sc[:, :T // 2].bitcast(I32), 0)
        nc.vector.memset(tab_sc[:, T // 2:].bitcast(I32), 0)
        nc.scalar.activation(zero[:], zero_in[:], ACT.Sin)
        nc.vector.memset(w4_sc[:].bitcast(I32), 0)
        nc.vector.memset(w6_sc[:].bitcast(I32), 0)
        nc.vector.memset(minus_offset[:], -TURN_OFFSET)

        w1_raw = {}

        def load_w1(a, g):
            raw = ring.tile([P, PACK, K_PASS], F32, name="raw", tag="raw", bufs=3)
            rows = w1[g * K_PASS:(g + 1) * K_PASS, a * K_PASS:(a + 1) * K_PASS]
            nc.sync.dma_start(raw[:], rows.rearrange("(p i) c -> p i c", i=PACK))
            w1_raw[a, g] = raw

        def load_tab(g):
            nc.sync.dma_start(tab[g][:].bitcast(I32), tab_words[g].rearrange("p n i -> p (n i)").bitcast(I32))

        def load_page(s):
            a, t = divmod(s, PACK)
            rows = page0[a * K_PASS:(a + 1) * K_PASS, :].rearrange("(p i) m -> p i m", i=PACK)
            nc.sync.dma_start(page[s][:], rows[:, t, :])

        def load_wgs(t, c0=0, c1=S):
            rows = wgs.rearrange("(q i) j -> q i j", i=PACK)[:, t, c0:c1]
            for q in (0, 2, 1, 3):
                nc.sync.dma_start(wgs_sb[t][32 * q:32 * (q + 1), c0:c1], rows)

        nc.sync.dma_start(idx_tab[:], offs)
        make_identity(nc, ident[:])
        nc.sync.dma_start(idx_put[:], offs2)
        nc.sync.dma_start(idx_get[:], offs3)
        nc.sync.dma_start(idx_out[:], offs4)
        nc.sync.dma_start(gain_sb[:], gain.rearrange("(a p i) -> p a i", p=P, i=PACK))
        nc.sync.dma_start(base_sb[:], base.rearrange("(a p i) -> p a i", p=P, i=PACK))
        load_w1(0, 0)
        load_tab(0)
        for q in range(4):
            nc.sync.dma_start(tab_sc[32 * q:32 * q + 4 * K_PASSES, :].bitcast(I32),
                              tab_scales[:, 4 * q:4 * q + 4, :].bitcast(I32))
        load_w1(0, 1)
        load_tab(1)
        load_w1(0, 2)
        load_tab(2)
        load_wgs(0, 0, HALF)
        load_page(0)
        load_wgs(0, HALF, S)
        load_wgs(1)
        load_page(1)
        load_w1(1, 0)
        load_w1(1, 1)
        load_wgs(2)
        load_page(2)
        load_w1(1, 2)
        load_wgs(3)
        load_page(3)

        def gather_words(g, c0, c1):
            nc.vector.tensor_copy(v_words[g][:, c0:c1], tab[g][:].indirect(idx_tab[:, c0 // 16:c1 // 16]))

        staged = {}

        def staging(key):
            if key not in staged:
                staged[key] = ring.tile([P, K_PASS * PACK], BF16, name="grouped", tag="grouped", bufs=3, align_bytes=64)
            return staged[key]

        follows = {(2, 0): ("w1", 1, 0), (3, 0): ("w1", 1, 2),
                   (5, 0): "w5", (6, 0): ("x", 0, 0), (7, 0): ("x", 0, 1)}

        def cast_w1(a, g):
            grouped = staging(("w1", a, g))
            nc.scalar.copy(grouped[:].rearrange("p (t m i) -> p m i t", t=PACK, i=PACK),
                           w1_raw[a, g][:].rearrange("p i (m t) -> p m i t", t=PACK))

        def quantize_w1(a, g):
            nc.vector.quantize_mx(w1_codes[a][g][:].bitcast(FP8X4), w1_sc[a][g][:], staging(("w1", a, g))[:])

        new_states = {}
        factors = {}

        def scratch(s, role):
            return work[(role + 3 * s) % 4]

        def first_product(s, c0, c1, z, angle, whole):
            a, t = divmod(s, PACK)
            blocks = (c1 - c0) // P
            for g in range(K_PASSES):
                for b in range(blocks):
                    cols = slice(c0 + b * P, c0 + (b + 1) * P)
                    nc.tensor.matmul_mx(
                        out=z[:, b * P:(b + 1) * P],
                        lhsT=v_words[g][:, cols].bitcast(FP8X4),
                        lhsT_scale=v_sc[4 * g:P, cols],
                        rhs=w1_codes[a][g][:, t * P:(t + 1) * P].bitcast(FP8X4),
                        rhs_scale=w1_sc[a][g][:, t * P:(t + 1) * P],
                        start=(g == 0 and b == 0),
                        stop=(g == K_PASSES - 1 and b == blocks - 1),
                    )
            if (s, c0) == (0, HALF):
                nc.vector.tensor_scalar(angle, z[:, :c1 - c0], 1.0 / (2.0 * math.pi), 0.25, ALU.mult, ALU.add)
                nc.vector.tensor_scalar(whole.bitcast(I32), angle, -BITS_PER_TURN, TURN_OFFSET_BITS, ALU.mult, ALU.add)
            else:
                nc.scalar.activation(angle, z[:, :c1 - c0], ACT.Copy, bias=0.25, scale=1.0 / (2.0 * math.pi))
                nc.scalar.activation(whole.bitcast(U32), angle, ACT.Copy, bias=TURN_OFFSET_BITS, scale=-BITS_PER_TURN)

        def cosine(s, c0, c1, frac, angle, whole):
            blocks = (c1 - c0) // P
            terms = [(b, minus_offset[:]) for b in range(blocks)]
            terms.extend((b, term[:, b * P:(b + 1) * P]) for b in range(blocks) for term in (whole, angle))
            for n, (b, term) in enumerate(terms):
                nc.tensor.matmul(frac[:, b * P:(b + 1) * P], term, ident[:], is_transpose=True,
                                 start=(n == 0), stop=(n == len(terms) - 1))
            nc.scalar.activation(new_states[s][:, c0:c1], frac[:, :c1 - c0], ACT.Sin, bias=zero[:], scale=2.0 * math.pi)

        def states(s, pieces):
            new_states[s] = ring.tile([P, S], F32, name="new_state", tag="new_state", align_bytes=64)
            a, t = divmod(s, PACK)
            factors[s] = shared.tile([P, S], F32, name=f"factor{s}", offset=(108 + 4 * (s % 2)) * KIB)
            for c0, c1 in ((0, HALF), (HALF, S)) if s == 0 else ((0, S),):
                nc.gpsimd.tensor_scalar(factors[s][:, c0:c1], wgs_sb[t][:, c0:c1], gain_sb[:, a, t:t + 1], 0.0,
                                        ALU.mult, ALU.add)
            jobs = []
            for c0, c1, z_bank, frac_bank in pieces:
                h, at = divmod(c0, HALF)
                angle = scratch(s, 3 * h)[:, at:at + c1 - c0]
                if (s, c0) == (2, 0):
                    angle = staging(("w1", 1, 1))[:].bitcast(F32)[:, :c1 - c0]
                if (s, c0) in follows:
                    whole = staging(follows[s, c0])[:].bitcast(F32)[:, :c1 - c0]
                else:
                    whole = scratch(s, 1 + h)[:, at:at + c1 - c0]
                first_product(s, c0, c1, bank(z_bank), angle, whole)
                jobs.append((c0, c1, frac_bank, angle, whole))
            for c0, c1, frac_bank, angle, whole in jobs:
                cosine(s, c0, c1, bank(frac_bank), angle, whole)

        def put(s, c0=0, c1=S):
            nc.vector.tensor_tensor(page[s][:].indirect(idx_put[:, c0 // 16:c1 // 16]),
                                    new_states[s][:, c0:c1], factors[s][:, c0:c1], ALU.mult)

        picked = {}
        rounded = {}

        def get(s, h, into):
            picked[s, h] = into
            nc.vector.tensor_copy(into, page[s][:].indirect(idx_get[:, h * 32:(h + 1) * 32]))

        def depart(s, h):
            a, t = divmod(s, PACK)
            if t == 0:
                rounded[a, h] = ring.tile([P, PACK, HALF], BF16, name="rounded", tag="rounded", bufs=4)
            nc.scalar.activation(rounded[a, h][:, t, :], picked[s, h], ACT.Identity, bias=neg_base[:, a, t:t + 1])

        woven = {}

        def weave(a, h):
            x_bf = staging(("x", a, h))
            nc.scalar.copy(x_bf[:].rearrange("p (c i t) -> p c t i", i=4, t=PACK),
                           rounded[a, h][:].rearrange("p t (c i) -> p c t i", i=4))
            woven[a, h] = x_bf

        def quantize_x(a, h):
            xq, xs, rq, rs = x_mx[a, h]
            if (a, h) == (0, 0):
                r_bf = new_states[SLICES - 1][:].bitcast(BF16)
            else:
                r_bf = ring.tile([P, HALF * PACK], BF16, name="raised", tag="raised", align_bytes=64)[:]
            nc.vector.tensor_scalar(r_bf, woven[a, h][:], -1.0, 0.0, ALU.mult, ALU.min)
            nc.vector.quantize_mx(xq[:].bitcast(FP8X4), xs[:], woven[a, h][:])
            nc.vector.quantize_mx(rq[:].bitcast(FP8X4), rs[:], r_bf)

        sums = {}

        def second_products(a, h, b):
            if a == 0:
                first = 4 * (1 - h) + 2 * b
                sums[h, b] = (bank(first), bank(first + 1))
            diff, third = sums[h, b]
            xq, xs, rq, rs = x_mx[a, h]
            cols = slice(a * N + b * P, a * N + (b + 1) * P)
            w4_cols = slice(2 * cols.start, 2 * cols.stop)
            last = a == H_PASSES - 1
            nc.tensor.matmul_mx(out=diff[:], lhsT=w4_sb[:, w4_cols].bitcast(FP4X4), lhsT_scale=w4_sc[:, cols],
                                rhs=xq[:].bitcast(FP8X4), rhs_scale=xs[:], start=(a == 0), stop=False)
            nc.tensor.matmul_mx(out=diff[:], lhsT=w5_codes[:, cols].bitcast(FP8X4), lhsT_scale=w5_sc[:, cols],
                                rhs=rq[:].bitcast(FP8X4), rhs_scale=rs[:], start=False, stop=last)
            nc.tensor.matmul_mx(out=third[:], lhsT=w6_sb[:, cols].bitcast(FP8X4), lhsT_scale=w6_sc[:, cols],
                                rhs=xq[:].bitcast(FP8X4), rhs_scale=xs[:], start=(a == 0), stop=last)

        scores = {}

        def score(h, b):
            diff, third = sums[h, b]
            gap = ring.tile([P, HALF], F32, name="gap", tag="gap")
            scores[h, b] = ring.tile([P, HALF], F32, name="y", tag="y", bufs=3)
            nc.scalar.activation(gap[:], diff[:], ACT.Abs, bias=zero[:])
            nc.vector.tensor_tensor(scores[h, b][:], gap[:], third[:], ALU.max)

        def put_score(h, b):
            nc.vector.tensor_tensor(result[b][:].indirect(idx_out[:, h * 32:(h + 1) * 32]),
                                    scores[h, b][:], wgo_sb[:, h * HALF:(h + 1) * HALF], ALU.mult)

        gather_words(0, 0, S)
        cast_w1(0, 0)
        nc.vector.tensor_copy(v_sc[:], tab_sc[:].indirect(idx_tab[:]))
        cast_w1(0, 1)
        quantize_w1(0, 0)
        gather_words(1, 0, S)
        quantize_w1(0, 1)
        cast_w1(0, 2)
        quantize_w1(0, 2)
        gather_words(2, 0, HALF)
        gather_words(2, HALF, S)
        nc.vector.tensor_scalar(neg_base[:], base_sb[:], -1.0, 0.0, ALU.mult, ALU.add)

        for s in range(PACK, SLICES):
            load_page(s)
        w5_raw = ring.tile([P, H_PASSES, PACK, N], F32, name="raw", tag="raw", bufs=3)
        nc.sync.dma_start(w5_raw[:], w5.rearrange("(a p i) n -> p a i n", p=P, i=PACK))
        nc.sync.dma_start(w4_sb[:].bitcast(I32).rearrange("p (a c) -> p a c", a=H_PASSES),
                          w4_words.bitcast(I32).rearrange("a p c -> p a c"))
        nc.sync.dma_start(w6_sb[:].bitcast(I32).rearrange("p (a c) -> p a c", a=H_PASSES),
                          w6_words.rearrange("a p c i -> p a (c i)").bitcast(I32))
        for q in range(4):
            for plane, scales in ((w4_sc, w4_scales), (w6_sc, w6_scales)):
                nc.sync.dma_start(
                    plane[32 * q:32 * q + 4, :].bitcast(I32).rearrange("r (a n) -> r a n", a=H_PASSES),
                    scales[:, 4 * q:4 * q + 4, :].bitcast(I32).rearrange("a r n -> r a n"))
        nc.sync.dma_start(wgo_sb[:], wgo)
        for b in range(N // P):
            nc.sync.dma_start(result[b][:], page1[b * P:(b + 1) * P, :])

        def halves_of_list(s):
            return [(h * HALF, (h + 1) * HALF, h + 2 * (2 * s % 3), h + 2 * ((2 * s + 1) % 3)) for h in range(2)]

        first_pieces = [(0, HALF // 2, 0, 2), (HALF // 2, HALF, 6, 7), (HALF, S, 1, 3)]
        states(0, first_pieces)
        for c0, c1, z_bank, frac_bank in first_pieces:
            put(0, c0, c1)
        states(1, halves_of_list(1))
        for s in range(1, SLICES):
            put(s)
            if s + 1 < SLICES:
                states(s + 1, halves_of_list(s + 1))
            if s == 1:
                cast_w1(1, 0)
                cast_w1(1, 1)
            if s == 2:
                cast_w1(1, 2)
            if s == PACK:
                w5_bf = staging("w5")
                nc.scalar.copy(w5_bf[:].rearrange("p (a c k i) -> p a c i k", a=H_PASSES, k=4, i=PACK),
                               w5_raw[:].rearrange("p a i (c k) -> p a c i k", k=4))
            if s in (PACK + 1, PACK + 2):
                weave(0, s - PACK - 1)
            if s + 1 < SLICES:
                for h in range(2):
                    get(s - 1, h, scratch(s + 1, 3 - h)[:])
                    depart(s - 1, h)
            if s == 1:
                quantize_w1(1, 0)
                quantize_w1(1, 1)
            if s == 2:
                quantize_w1(1, 2)
            if s == PACK:
                nc.vector.quantize_mx(w5_codes[:].bitcast(FP8X4), w5_sc[:], staging("w5")[:])
        for h in range(2):
            get(SLICES - 2, h, scratch(SLICES - 1, 3 - h)[:])
            depart(SLICES - 2, h)
            get(SLICES - 1, h, scratch(SLICES - 1, h)[:])
            depart(SLICES - 1, h)
            weave(1, h)
            quantize_x(h, 0)
            for b in range(N // P):
                second_products(h, 0, b)
        for a in range(H_PASSES):
            quantize_x(a, 1)
            for b in range(N // P):
                second_products(a, 1, b)
        parts = [(h, b) for h in range(2) for b in range(N // P)]
        score(*parts[0])
        for n, part in enumerate(parts):
            if n + 1 < len(parts):
                score(*parts[n + 1])
            put_score(*part)
        for b in range(N // P):
            nc.sync.dma_start(out[b * P:(b + 1) * P, :], result[b][:])
